import numpy as np
import ml_dtypes


def mxq(x, axis, fmt="e4m3"):
    dtype, down = {"e4m3": (ml_dtypes.float8_e4m3fn, 7), "e5m2": (ml_dtypes.float8_e5m2, 14)}[fmt]
    v = np.moveaxis(np.asarray(x, np.float32).astype(ml_dtypes.bfloat16).astype(np.float64), axis, -1)
    blocks = v.reshape(v.shape[:-1] + (-1, 32))
    amax = np.abs(blocks).max(-1, keepdims=True)
    byte = np.maximum(np.where(amax > 0, np.frexp(amax)[1] - 1 + 127, 0) - down, 1)
    scale = np.exp2(byte - 127.0)
    codes = (blocks / scale).astype(np.float32).astype(dtype).astype(np.float64)
    return np.moveaxis((codes * scale).reshape(v.shape), -1, axis)


WIDE = False


def mx_kscale(k):
    if not WIDE:
        return np.ones(k)
    levels = np.array([10, -10, 5, -5, 0])
    if k % 512:
        return np.exp2(np.random.permutation(np.resize(levels, k // 32))).repeat(32)
    a = np.empty((k // 512, 16))
    for p in range(k // 512):
        a[p, :8] = np.random.permutation(np.resize(levels, 8))
        for g in range(8):
            far = levels[np.abs(levels - a[p, g]) >= 10]
            a[p, g + 8] = far[np.random.randint(len(far))]
    return np.exp2(a.ravel()).repeat(32)


def f64(x):
    return np.asarray(x).astype(np.float64)


def striped(idx):
    return np.tile(idx.reshape(-1, 16).T, (8, 1)).astype(np.uint16)


def unstriped(offs):
    return offs[:16].T.reshape(-1).astype(np.int64)


def striped8(idx):
    return np.concatenate([x.reshape(-1, 16).T for x in idx]).astype(np.uint16)


def runs(offs, k):
    lists = np.stack([offs[16 * r : 16 * r + 16].T.reshape(-1) for r in range(8)]).astype(np.int64)
    return lists[np.arange(k) % 512 // 64]


def pack_weight(w):
    k, n = w.shape
    w = f64(np.asarray(w, np.float32).astype(ml_dtypes.bfloat16)).reshape(k // 32, 32, n)
    amax = np.abs(w).max(1)
    byte = np.clip(np.where(amax > 0, np.frexp(amax)[1] - 1 + 127 - 7, 1), 1, 254)
    scaled = (w * np.exp2(127.0 - byte)[:, None, :]).reshape(k, n).astype(np.float32)
    words = np.ascontiguousarray(scaled.reshape(k // 512, 128, 4, n).transpose(0, 1, 3, 2)).astype(ml_dtypes.float8_e4m3fn).view(np.uint8)
    return words, np.ascontiguousarray(byte.astype(np.uint8).reshape(k // 512, 16, n))


def unpack_weight(words, scales):
    g, p, n, _ = words.shape
    vals = np.ascontiguousarray(words).view(ml_dtypes.float8_e4m3fn).astype(np.float64) * np.repeat(np.exp2(scales.astype(np.float64) - 127.0), 8, axis=1)[..., None]
    return vals.transpose(0, 1, 3, 2).reshape(g * 512, n)

def planes(y):
    n, m = y.shape
    v = y.astype(np.float32).astype(ml_dtypes.bfloat16).astype(np.float64).reshape(n // 32, 32, m)
    top = np.abs(v).max(1)
    byte = np.clip(np.where(top > 0, np.frexp(top)[1] - 1 + 127 - 7, 1), 1, 254)
    codes = (v * np.exp2(127.0 - byte)[:, None, :]).reshape(n, m).astype(np.float32).astype(ml_dtypes.float8_e4m3fn).view(np.uint8)
    words = codes.reshape(n // 512, 128, 4, m).transpose(0, 1, 3, 2)
    return np.ascontiguousarray(words), np.ascontiguousarray(byte.astype(np.uint8).reshape(n // 512, 16, m))


K, T, S, N, H, W = 512, 2048, 256, 512, 512, 1024


def setup_inputs():
    n = np.random.standard_normal
    s = mx_kscale(K)[:, None]
    u = mx_kscale(H)
    packed_xT = pack_weight(n((K, T)) * s)
    packed_w1 = pack_weight(n((K, H)) / np.sqrt(K) / s)
    packed_w2 = pack_weight(n((H, N)) / np.sqrt(2 * H) / u[:, None])
    packed_w3 = pack_weight(n((K, N)) / np.sqrt(2 * K) / s)
    return {
        "x_words": packed_xT[0],
        "x_scales": packed_xT[1],
        "w1_words": packed_w1[0],
        "w1_scales": packed_w1[1],
        "gn": (np.random.uniform(0.5, 1.5, (H, 1)) * u[:, None]).astype(np.float32),
        "w2_words": packed_w2[0],
        "w2_scales": packed_w2[1],
        "w3_words": packed_w3[0],
        "w3_scales": packed_w3[1],
        "tau": np.random.uniform(0.3, 0.9, (N, 1)).astype(np.float32),
        "offs": striped(np.random.permutation(T)[:S]),
        "n1": striped(np.random.randint(0, S, W)),
        "two": striped(np.random.permutation(T)[:S]),
        "n2": striped8(np.stack([np.random.permutation(S) for _ in range(8)])),
        "n3": striped8(np.stack([np.random.permutation(S) for _ in range(8)])),
    }


def reference(x_words, x_scales, w1_words, w1_scales, gn, w2_words, w2_scales, w3_words, w3_scales, tau, offs, n1, two, n2, n3):
    xq = unpack_weight(x_words, x_scales)[:, unstriped(offs)]
    y = unpack_weight(w1_words, w1_scales).T @ xq
    ex = np.exp(y)
    mb = ex[:, unstriped(n1)]
    ms = mb.reshape(H, S, 4).sum(axis=2)
    z = f64(gn) * (np.log(ms + ex) - y)
    x_two = unpack_weight(x_words, x_scales)[:, unstriped(two)]
    h = unpack_weight(w2_words, w2_scales).T @ mxq(z, 0, "e4m3") + unpack_weight(w3_words, w3_scales).T @ x_two
    top = h.max(axis=1, keepdims=True)
    ea = np.exp(f64(tau) * (h[np.arange(N)[:, None], runs(n2, N)] - top))
    out_0 = np.maximum(h, 2.0 * ea) - (0.5 * (h[np.arange(N)[:, None], runs(n3, N)]))
    return (out_0,) + planes(out_0)

@@ -1,0 +1,228 @@
+from contextlib import ExitStack
+
+import concourse.mybir as mybir
+
+K, T, S, N, H, W = 512, 2048, 256, 512, 512, 1024
+FLOPS = 3 * 2 * 512 * 512 * 256
+
+F32 = mybir.dt.float32
+BF16 = mybir.dt.bfloat16
+U32 = mybir.dt.uint32
+I32 = mybir.dt.int32
+U16 = mybir.dt.uint16
+U8 = mybir.dt.uint8
+FP8X4 = mybir.dt.float8_e4m3fn_x4
+ALU = mybir.AluOpType
+ACT = mybir.ActivationFunctionType
+
+P = 128
+PACK = 4
+HALF = S // 2
+MEMBERS = 4
+EX_WINDOW = MEMBERS * HALF + 16
+
+
+def tile_picked_mixinglseecl_none_po_kernel(
+    tc, x_words, x_scales, w1_words, w1_scales, gn, w2_words, w2_scales, w3_words, w3_scales, tau, offs, n1, two, n2, n3, out_0, out_1, out_2
+):
+    nc = tc.nc
+    with ExitStack() as ctx:
+        keep = ctx.enter_context(tc.tile_pool(name="keep", bufs=1))
+        psum = ctx.enter_context(tc.psum_pool(name="psum", bufs=1))
+
+        def sb(name, shape, dtype):
+            return keep.tile(shape, dtype, name=name, align_bytes=64)
+
+        def load_words(queue, name, words):
+            raw = sb(name, [P, words.shape[2]], U32)
+            queue.dma_start(out=raw[:].bitcast(I32), in_=words[0].rearrange("p n t -> p (n t)").bitcast(I32))
+            return raw
+
+        def load_list(name, values):
+            listed = keep.tile(list(values.shape), U16, name=name)
+            nc.sync.dma_start(listed[:], values)
+            return listed
+
+        def load_scale_rows(queue, plane, first, scales, quad):
+            queue.dma_start(
+                out=plane[32 * quad + first : 32 * quad + first + 4, :].bitcast(I32),
+                in_=scales[0, 4 * quad : 4 * quad + 4, :].bitcast(I32),
+            )
+
+        def dealt(ap):
+            return ap.rearrange("p (t m) -> p m t", t=PACK)
+
+        def plain(ap):
+            return ap.rearrange("p (m t) -> p m t", t=PACK)
+
+        xs = sb("xs", [P, T], U8)
+        ws_raw = sb("ws_raw", [P, H], U8)
+        nc.vector.memset(xs[:].bitcast(I32), 0)
+
+        offs_sb = load_list("offs_sb", offs)
+        w1_raw = load_words(nc.scalar, "w_raw", w1_words)
+        for quad in range(4):
+            rows = w1_scales[0, 4 * quad : 4 * quad + 4, :].bitcast(I32)
+            nc.sync.dma_start(out=ws_raw[32 * quad : 32 * quad + 32, :].bitcast(I32), in_=rows.unsqueeze(0).to_broadcast([8, 4, H // 4]))
+        xw = load_words(nc.scalar, "xw", x_words)
+        for quad in range(4):
+            load_scale_rows(nc.sync, xs, 0, x_scales, quad)
+        two_sb = load_list("two_sb", two)
+        n1_sb = load_list("n1_sb", n1)
+        gn_sb = sb("gn_sb", [P, PACK], F32)
+        nc.gpsimd.dma_start(out=gn_sb[:], in_=gn.rearrange("(p t) o -> p (t o)", t=PACK))
+        tau_sb = sb("tau_sb", [P, PACK], F32)
+        nc.gpsimd.dma_start(out=tau_sb[:], in_=tau.rearrange("(p t) o -> p (t o)", t=PACK))
+        n2_sb = load_list("n2_sb", n2)
+        n3_sb = load_list("n3_sb", n3)
+
+        ex = [sb(f"ex{t}", [P, EX_WINDOW], F32) for t in range(PACK)]
+        for t in range(PACK):
+            nc.vector.memset(ex[t][:, S:], 0.0)
+
+        w1c = sb("w1c", [P, H], U32)
+        nc.vector.tensor_copy(out=dealt(w1c[:]), in_=plain(w1_raw[:]))
+        w1s = sb("w1s", [P, H], U8)
+        nc.vector.tensor_copy(out=dealt(w1s[:]), in_=plain(ws_raw[:]))
+        w23_raw = sb("w_raw", [P, 2 * N], U32)
+        for i, words in enumerate((w3_words, w2_words)):
+            nc.sync.dma_start(out=w23_raw[:, i * N : (i + 1) * N].bitcast(I32), in_=words[0].rearrange("p n t -> p (n t)").bitcast(I32))
+        for quad in range(4):
+            load_scale_rows(nc.sync, ws_raw, 4, w3_scales, quad)
+            load_scale_rows(nc.sync, ws_raw, 0, w2_scales, quad)
+        xq_w = sb("xq_w", [P, S], U32)
+        nc.vector.tensor_copy(xq_w[:], xw[:].indirect(offs_sb[:]))
+        xq_s = sb("xq_s", [P, S], U8)
+        nc.vector.tensor_copy(xq_s[:], xs[:].indirect(offs_sb[:]))
+        x2_w = sb("x2_w", [P, S], U32)
+        nc.vector.tensor_copy(x2_w[:], xw[:].indirect(two_sb[:]))
+        x2_s = sb("x2_s", [P, S], U8)
+        nc.vector.tensor_copy(x2_s[:], xs[:].indirect(two_sb[:]))
+
+        y_ps = [psum.tile([P, S], F32, name=f"y{t}") for t in range(PACK)]
+        h_ps = [psum.tile([P, S], F32, name=f"h{t}") for t in range(PACK)]
+        cols = [slice(P * t, P * (t + 1)) for t in range(PACK)]
+        for t in range(PACK):
+            nc.tensor.matmul_mx(
+                out=y_ps[t][:], lhsT=w1c[:, cols[t]].bitcast(FP8X4), lhsT_scale=w1s[:, cols[t]],
+                rhs=xq_w[:].bitcast(FP8X4), rhs_scale=xq_s[:], start=True, stop=True,
+            )
+        for t in range(PACK):
+            nc.scalar.activation(out=ex[t][:, :S], in_=y_ps[t][:], func=ACT.Exp)
+        w3c = sb("w3c", [P, N], U32)
+        inv = sb("inv", [P, PACK, S], F32)
+
+        groups = [[(0, 1), (2, 3)], [(0, 1), (2, 3)]]
+        on_vector = [[32, 32, 32, 32], [0, 0, 0, 0]]
+        list_cols = MEMBERS * HALF // 16
+        w2c = sb("w2c", [P, N], U32)
+        w23s = sb("w23s", [P, N], U8)
+        zq = [sb(f"zq{half}", [P, HALF], U32) for half in range(2)]
+        zs = [sb(f"zs{half}", [P, HALF], U8) for half in range(2)]
+        logs = [sb(f"logs{half}", [P, PACK, HALF], F32) for half in range(2)]
+        ratio = {}
+
+        def gather(half, which):
+            for group in which:
+                mb = sb(f"mb{half}_{group[0]}", [P, len(group), MEMBERS * HALF], F32)
+                for i, t in enumerate(group):
+                    first = half * list_cols
+                    split = on_vector[half][t]
+                    if split > 0:
+                        nc.vector.tensor_copy(mb[:, i, : 16 * split], ex[t][:].indirect(n1_sb[:, first : first + split]))
+                    if split < list_cols:
+                        nc.scalar.activation(mb[:, i, 16 * split :], ex[t][:].indirect(n1_sb[:, first + split : first + list_cols]), ACT.Copy)
+                ratio[half, group] = mb
+
+        def sums(half):
+            pairs, total = {}, {}
+            for group in groups[half]:
+                pairs[group] = sb(f"pairs{half}_{group[0]}", [P, len(group) * HALF, 2], F32)
+                members = ratio[half, group][:].rearrange("p g (j m) -> p (g j) m", m=MEMBERS)
+                nc.vector.tensor_tensor(pairs[group][:], members[:, :, 0:2], members[:, :, 2:4], ALU.add)
+            for group in groups[half]:
+                total[group] = sb(f"total{half}_{group[0]}", [P, len(group) * HALF], F32)
+                nc.vector.tensor_tensor(total[group][:], pairs[group][:, :, 0], pairs[group][:, :, 1], ALU.add)
+            for group in groups[half]:
+                r = sb(f"ratio{half}_{group[0]}", [P, len(group), HALF], F32)
+                nc.vector.tensor_tensor(
+                    r[:], total[group][:].rearrange("p (g j) -> p g j", j=HALF),
+                    inv[:, group[0] : group[-1] + 1, half * HALF : (half + 1) * HALF], ALU.mult,
+                )
+                ratio[half, group] = r
+
+        def logarithm(half):
+            for group in groups[half]:
+                nc.scalar.activation(out=logs[half][:, group[0] : group[-1] + 1, :], in_=ratio[half, group][:], func=ACT.Ln, bias=1.0)
+
+        def quantise_z(half):
+            zb = sb(f"zb{half}", [P, HALF, PACK], BF16)
+            nc.vector.tensor_tensor(
+                zb[:], logs[half][:].rearrange("p t j -> p j t"), gn_sb[:].unsqueeze(1).to_broadcast([P, HALF, PACK]), ALU.mult
+            )
+            nc.vector.quantize_mx(out=zq[half][:].bitcast(FP8X4), scales=zs[half][:], in_=zb[:].rearrange("p j t -> p (j t)"))
+
+        def second_product(half):
+            for t in range(PACK):
+                nc.tensor.matmul_mx(
+                    out=h_ps[t][:, half * HALF : (half + 1) * HALF], lhsT=w2c[:, cols[t]].bitcast(FP8X4), lhsT_scale=w23s[:, cols[t]],
+                    rhs=zq[half][:].bitcast(FP8X4), rhs_scale=zs[half][:], start=False, stop=(half == 1),
+                )
+
+        gather(0, groups[0])
+        gather(1, groups[1][:1])
+        minus_tau = sb("minus_tau", [P, PACK], F32)
+        nc.scalar.activation(out=minus_tau[:], in_=tau_sb[:], func=ACT.Copy, scale=-1.0)
+        for t in range(PACK):
+            nc.scalar.activation(out=inv[:, t, :], in_=y_ps[t][:], func=ACT.Exp, scale=-1.0)
+        gather(1, groups[1][1:])
+        nc.gpsimd.tensor_copy(out=dealt(w3c[:]), in_=plain(w23_raw[:, :N]))
+        nc.gpsimd.tensor_copy(out=dealt(w2c[:]), in_=plain(w23_raw[:, N:]))
+        nc.gpsimd.tensor_copy(out=dealt(w23s[:]), in_=plain(ws_raw[:]))
+        sums(0)
+        for t in range(PACK):
+            nc.tensor.matmul_mx(
+                out=h_ps[t][:], lhsT=w3c[:, cols[t]].bitcast(FP8X4), lhsT_scale=w23s[4:P, cols[t]],
+                rhs=x2_w[:].bitcast(FP8X4), rhs_scale=x2_s[:], start=True, stop=False,
+            )
+        logarithm(0)
+        sums(1)
+        quantise_z(0)
+        second_product(0)
+        logarithm(1)
+        quantise_z(1)
+        second_product(1)
+
+        h = [sb(f"h_sb{t}", [P, S], F32) for t in range(PACK)]
+        top = [sb(f"top{t}", [P, 1], F32) for t in range(PACK)]
+        shift = [sb(f"shift{t}", [P, 1], F32) for t in range(PACK)]
+        for t in range(PACK):
+            nc.vector.tensor_scalar(out=h[t][:], in0=h_ps[t][:], scalar1=1.0, scalar2=None, op0=ALU.mult, op1=ALU.max, accum_out=top[t][:])
+            nc.vector.tensor_scalar(out=shift[t][:], in0=top[t][:], scalar1=minus_tau[:, t : t + 1], scalar2=None, op0=ALU.mult)
+
+        other = [sb(f"top{t}", [P, S], F32) for t in range(PACK)]
+        codes = sb("codes", [P, S], U32)
+        code_scales = sb("code_scales", [P, S], U8)
+        out_rows = out_0.rearrange("(p t) j -> p t j", t=PACK)
+        out_words = out_1[0].rearrange("p n t -> p (n t)").bitcast(I32)
+        for half in range(2):
+            js = slice(half * HALF, (half + 1) * HALF)
+            ls = slice(half * HALF // 16, (half + 1) * HALF // 16)
+            result = sb(f"result{half}", [P, PACK, HALF], F32)
+            for t in range(PACK):
+                ea = sb(f"ea{half}_{t}", [P, HALF], F32)
+                nc.scalar.activation(ea[:], h[t][:].indirect(n2_sb[:, ls]), ACT.Exp, bias=shift[t][:], scale=tau_sb[:, t : t + 1])
+                nc.scalar.activation(other[t][:, js], h[t][:].indirect(n3_sb[:, ls]), ACT.Copy)
+                larger = sb(f"larger{half}_{t}", [P, HALF], F32)
+                nc.vector.scalar_tensor_tensor(larger[:], ea[:], 2.0, h[t][:, js], ALU.mult, ALU.max)
+                nc.vector.scalar_tensor_tensor(result[:, t, :], other[t][:, js], -0.5, larger[:], ALU.mult, ALU.add)
+            nc.sync.dma_start(out=out_rows[:, :, js], in_=result[:])
+            rounded = sb(f"rounded{half}", [P, HALF, PACK], BF16)
+            nc.vector.tensor_copy(out=rounded[:], in_=result[:].rearrange("p t j -> p j t"))
+            nc.vector.quantize_mx(out=codes[:, js].bitcast(FP8X4), scales=code_scales[:, js], in_=rounded[:].rearrange("p j t -> p (j t)"))
+            nc.sync.dma_start(out=out_words[:, js], in_=codes[:, js].bitcast(I32))
+        for quad in range(4):
+            queue = nc.scalar if quad < 2 else nc.sync
+            queue.dma_start(
+                out=out_2[0, 4 * quad : 4 * quad + 4, :].bitcast(I32), in_=code_scales[32 * quad : 32 * quad + 4, :].bitcast(I32)
+            )

@@ -80,6 +80,10 @@ def tile_picked_mixinglseecl_none_po_kernel(
         for t in range(PACK):
             nc.vector.memset(ex[t][:, S:], 0.0)
 
+        h = [sb(f"h_sb{t}", [P, 2 * S], F32) for t in range(PACK)]
+        for t in range(PACK):
+            nc.vector.memset(h[t][:, S:], 0.0)
+
         w1c = sb("w1c", [P, H], U32)
         nc.vector.tensor_copy(out=dealt(w1c[:]), in_=plain(w1_raw[:]))
         w1s = sb("w1s", [P, H], U8)
@@ -193,14 +197,18 @@ def tile_picked_mixinglseecl_none_po_kernel(
         quantise_z(1)
         second_product(1)
 
-        h = [sb(f"h_sb{t}", [P, S], F32) for t in range(PACK)]
         top = [sb(f"top{t}", [P, 1], F32) for t in range(PACK)]
         shift = [sb(f"shift{t}", [P, 1], F32) for t in range(PACK)]
         for t in range(PACK):
-            nc.vector.tensor_scalar(out=h[t][:], in0=h_ps[t][:], scalar1=1.0, scalar2=None, op0=ALU.mult, op1=ALU.max, accum_out=top[t][:])
+            nc.vector.tensor_scalar(out=h[t][:, :S], in0=h_ps[t][:], scalar1=1.0, scalar2=None, op0=ALU.mult, op1=ALU.max, accum_out=top[t][:])
             nc.vector.tensor_scalar(out=shift[t][:], in0=top[t][:], scalar1=minus_tau[:, t : t + 1], scalar2=None, op0=ALU.mult)
 
-        other = [sb(f"top{t}", [P, S], F32) for t in range(PACK)]
+        larger = [sb(f"larger{t}", [P, S], F32) for t in range(PACK)]
+        for t in range(PACK):
+            ea = sb(f"ea{t}", [P, S], F32)
+            nc.scalar.activation(ea[:], h[t][:].indirect(n2_sb[:]), ACT.Exp, bias=shift[t][:], scale=tau_sb[:, t : t + 1])
+            nc.vector.scalar_tensor_tensor(larger[t][:], ea[:], 2.0, h[t][:, :S], ALU.mult, ALU.max)
+        other = sb(f"top{PACK - 1}", [P, 2, PACK, HALF], F32)
         codes = sb("codes", [P, S], U32)
         code_scales = sb("code_scales", [P, S], U8)
         out_rows = out_0.rearrange("(p t) j -> p t j", t=PACK)
@@ -210,12 +218,8 @@ def tile_picked_mixinglseecl_none_po_kernel(
             ls = slice(half * HALF // 16, (half + 1) * HALF // 16)
             result = sb(f"result{half}", [P, PACK, HALF], F32)
             for t in range(PACK):
-                ea = sb(f"ea{half}_{t}", [P, HALF], F32)
-                nc.scalar.activation(ea[:], h[t][:].indirect(n2_sb[:, ls]), ACT.Exp, bias=shift[t][:], scale=tau_sb[:, t : t + 1])
-                nc.scalar.activation(other[t][:, js], h[t][:].indirect(n3_sb[:, ls]), ACT.Copy)
-                larger = sb(f"larger{half}_{t}", [P, HALF], F32)
-                nc.vector.scalar_tensor_tensor(larger[:], ea[:], 2.0, h[t][:, js], ALU.mult, ALU.max)
-                nc.vector.scalar_tensor_tensor(result[:, t, :], other[t][:, js], -0.5, larger[:], ALU.mult, ALU.add)
+                nc.scalar.activation(other[:, half, t, :], h[t][:].indirect(n3_sb[:, ls]), ACT.Copy)
+                nc.vector.scalar_tensor_tensor(result[:, t, :], other[:, half, t, :], -0.5, larger[t][:, js], ALU.mult, ALU.add)
             nc.sync.dma_start(out=out_rows[:, :, js], in_=result[:])
             rounded = sb(f"rounded{half}", [P, HALF, PACK], BF16)
             nc.vector.tensor_copy(out=rounded[:], in_=result[:].rearrange("p t j -> p j t"))

from contextlib import ExitStack

import concourse.mybir as mybir

K, T, S, N, H, W = 512, 2048, 256, 512, 512, 1024
FLOPS = 3 * 2 * 512 * 512 * 256

F32 = mybir.dt.float32
BF16 = mybir.dt.bfloat16
U32 = mybir.dt.uint32
I32 = mybir.dt.int32
U16 = mybir.dt.uint16
U8 = mybir.dt.uint8
FP8X4 = mybir.dt.float8_e4m3fn_x4
ALU = mybir.AluOpType
ACT = mybir.ActivationFunctionType

P = 128
PACK = 4
HALF = S // 2
MEMBERS = 4
EX_WINDOW = MEMBERS * HALF + 16


def tile_picked_mixinglseecl_none_po_kernel(
    tc, x_words, x_scales, w1_words, w1_scales, gn, w2_words, w2_scales, w3_words, w3_scales, tau, offs, n1, two, n2, n3, out_0, out_1, out_2
):
    nc = tc.nc
    with ExitStack() as ctx:
        keep = ctx.enter_context(tc.tile_pool(name="keep", bufs=1))
        psum = ctx.enter_context(tc.psum_pool(name="psum", bufs=1))

        def sb(name, shape, dtype):
            return keep.tile(shape, dtype, name=name, align_bytes=64)

        def load_words(queue, name, words):
            raw = sb(name, [P, words.shape[2]], U32)
            queue.dma_start(out=raw[:].bitcast(I32), in_=words[0].rearrange("p n t -> p (n t)").bitcast(I32))
            return raw

        def load_list(name, values):
            listed = keep.tile(list(values.shape), U16, name=name)
            nc.sync.dma_start(listed[:], values)
            return listed

        def load_scale_rows(queue, plane, first, scales, quad):
            queue.dma_start(
                out=plane[32 * quad + first : 32 * quad + first + 4, :].bitcast(I32),
                in_=scales[0, 4 * quad : 4 * quad + 4, :].bitcast(I32),
            )

        def dealt(ap):
            return ap.rearrange("p (t m) -> p m t", t=PACK)

        def plain(ap):
            return ap.rearrange("p (m t) -> p m t", t=PACK)

        xs = sb("xs", [P, T], U8)
        ws_raw = sb("ws_raw", [P, H], U8)
        nc.vector.memset(xs[:].bitcast(I32), 0)

        offs_sb = load_list("offs_sb", offs)
        w1_raw = load_words(nc.scalar, "w_raw", w1_words)
        for quad in range(4):
            rows = w1_scales[0, 4 * quad : 4 * quad + 4, :].bitcast(I32)
            nc.sync.dma_start(out=ws_raw[32 * quad : 32 * quad + 32, :].bitcast(I32), in_=rows.unsqueeze(0).to_broadcast([8, 4, H // 4]))
        xw = load_words(nc.scalar, "xw", x_words)
        for quad in range(4):
            load_scale_rows(nc.sync, xs, 0, x_scales, quad)
        two_sb = load_list("two_sb", two)
        n1_sb = load_list("n1_sb", n1)
        gn_sb = sb("gn_sb", [P, PACK], F32)
        nc.gpsimd.dma_start(out=gn_sb[:], in_=gn.rearrange("(p t) o -> p (t o)", t=PACK))
        tau_sb = sb("tau_sb", [P, PACK], F32)
        nc.gpsimd.dma_start(out=tau_sb[:], in_=tau.rearrange("(p t) o -> p (t o)", t=PACK))
        n2_sb = load_list("n2_sb", n2)
        n3_sb = load_list("n3_sb", n3)

        ex = [sb(f"ex{t}", [P, EX_WINDOW], F32) for t in range(PACK)]
        for t in range(PACK):
            nc.vector.memset(ex[t][:, S:], 0.0)

        h = [sb(f"h_sb{t}", [P, 2 * S], F32) for t in range(PACK)]
        for t in range(PACK):
            nc.vector.memset(h[t][:, S:], 0.0)

        w1c = sb("w1c", [P, H], U32)
        nc.vector.tensor_copy(out=dealt(w1c[:]), in_=plain(w1_raw[:]))
        w1s = sb("w1s", [P, H], U8)
        nc.vector.tensor_copy(out=dealt(w1s[:]), in_=plain(ws_raw[:]))
        w23_raw = sb("w_raw", [P, 2 * N], U32)
        for i, words in enumerate((w3_words, w2_words)):
            nc.sync.dma_start(out=w23_raw[:, i * N : (i + 1) * N].bitcast(I32), in_=words[0].rearrange("p n t -> p (n t)").bitcast(I32))
        for quad in range(4):
            load_scale_rows(nc.sync, ws_raw, 4, w3_scales, quad)
            load_scale_rows(nc.sync, ws_raw, 0, w2_scales, quad)
        xq_w = sb("xq_w", [P, S], U32)
        nc.vector.tensor_copy(xq_w[:], xw[:].indirect(offs_sb[:]))
        xq_s = sb("xq_s", [P, S], U8)
        nc.vector.tensor_copy(xq_s[:], xs[:].indirect(offs_sb[:]))
        x2_w = sb("x2_w", [P, S], U32)
        nc.vector.tensor_copy(x2_w[:], xw[:].indirect(two_sb[:]))
        x2_s = sb("x2_s", [P, S], U8)
        nc.vector.tensor_copy(x2_s[:], xs[:].indirect(two_sb[:]))

        y_ps = [psum.tile([P, S], F32, name=f"y{t}") for t in range(PACK)]
        h_ps = [psum.tile([P, S], F32, name=f"h{t}") for t in range(PACK)]
        cols = [slice(P * t, P * (t + 1)) for t in range(PACK)]
        for t in range(PACK):
            nc.tensor.matmul_mx(
                out=y_ps[t][:], lhsT=w1c[:, cols[t]].bitcast(FP8X4), lhsT_scale=w1s[:, cols[t]],
                rhs=xq_w[:].bitcast(FP8X4), rhs_scale=xq_s[:], start=True, stop=True,
            )
        for t in range(PACK):
            nc.scalar.activation(out=ex[t][:, :S], in_=y_ps[t][:], func=ACT.Exp)
        w3c = sb("w3c", [P, N], U32)
        inv = sb("inv", [P, PACK, S], F32)

        groups = [[(0, 1), (2, 3)], [(0, 1), (2, 3)]]
        on_vector = [[32, 32, 32, 32], [0, 0, 0, 0]]
        list_cols = MEMBERS * HALF // 16
        w2c = sb("w2c", [P, N], U32)
        w23s = sb("w23s", [P, N], U8)
        zq = [sb(f"zq{half}", [P, HALF], U32) for half in range(2)]
        zs = [sb(f"zs{half}", [P, HALF], U8) for half in range(2)]
        logs = [sb(f"logs{half}", [P, PACK, HALF], F32) for half in range(2)]
        ratio = {}

        def gather(half, which):
            for group in which:
                mb = sb(f"mb{half}_{group[0]}", [P, len(group), MEMBERS * HALF], F32)
                for i, t in enumerate(group):
                    first = half * list_cols
                    split = on_vector[half][t]
                    if split > 0:
                        nc.vector.tensor_copy(mb[:, i, : 16 * split], ex[t][:].indirect(n1_sb[:, first : first + split]))
                    if split < list_cols:
                        nc.scalar.activation(mb[:, i, 16 * split :], ex[t][:].indirect(n1_sb[:, first + split : first + list_cols]), ACT.Copy)
                ratio[half, group] = mb

        def sums(half):
            pairs, total = {}, {}
            for group in groups[half]:
                pairs[group] = sb(f"pairs{half}_{group[0]}", [P, len(group) * HALF, 2], F32)
                members = ratio[half, group][:].rearrange("p g (j m) -> p (g j) m", m=MEMBERS)
                nc.vector.tensor_tensor(pairs[group][:], members[:, :, 0:2], members[:, :, 2:4], ALU.add)
            for group in groups[half]:
                total[group] = sb(f"total{half}_{group[0]}", [P, len(group) * HALF], F32)
                nc.vector.tensor_tensor(total[group][:], pairs[group][:, :, 0], pairs[group][:, :, 1], ALU.add)
            for group in groups[half]:
                r = sb(f"ratio{half}_{group[0]}", [P, len(group), HALF], F32)
                nc.vector.tensor_tensor(
                    r[:], total[group][:].rearrange("p (g j) -> p g j", j=HALF),
                    inv[:, group[0] : group[-1] + 1, half * HALF : (half + 1) * HALF], ALU.mult,
                )
                ratio[half, group] = r

        def logarithm(half):
            for group in groups[half]:
                nc.scalar.activation(out=logs[half][:, group[0] : group[-1] + 1, :], in_=ratio[half, group][:], func=ACT.Ln, bias=1.0)

        def quantise_z(half):
            zb = sb(f"zb{half}", [P, HALF, PACK], BF16)
            nc.vector.tensor_tensor(
                zb[:], logs[half][:].rearrange("p t j -> p j t"), gn_sb[:].unsqueeze(1).to_broadcast([P, HALF, PACK]), ALU.mult
            )
            nc.vector.quantize_mx(out=zq[half][:].bitcast(FP8X4), scales=zs[half][:], in_=zb[:].rearrange("p j t -> p (j t)"))

        def second_product(half):
            for t in range(PACK):
                nc.tensor.matmul_mx(
                    out=h_ps[t][:, half * HALF : (half + 1) * HALF], lhsT=w2c[:, cols[t]].bitcast(FP8X4), lhsT_scale=w23s[:, cols[t]],
                    rhs=zq[half][:].bitcast(FP8X4), rhs_scale=zs[half][:], start=False, stop=(half == 1),
                )

        gather(0, groups[0])
        gather(1, groups[1][:1])
        minus_tau = sb("minus_tau", [P, PACK], F32)
        nc.scalar.activation(out=minus_tau[:], in_=tau_sb[:], func=ACT.Copy, scale=-1.0)
        for t in range(PACK):
            nc.scalar.activation(out=inv[:, t, :], in_=y_ps[t][:], func=ACT.Exp, scale=-1.0)
        gather(1, groups[1][1:])
        nc.gpsimd.tensor_copy(out=dealt(w3c[:]), in_=plain(w23_raw[:, :N]))
        nc.gpsimd.tensor_copy(out=dealt(w2c[:]), in_=plain(w23_raw[:, N:]))
        nc.gpsimd.tensor_copy(out=dealt(w23s[:]), in_=plain(ws_raw[:]))
        sums(0)
        for t in range(PACK):
            nc.tensor.matmul_mx(
                out=h_ps[t][:], lhsT=w3c[:, cols[t]].bitcast(FP8X4), lhsT_scale=w23s[4:P, cols[t]],
                rhs=x2_w[:].bitcast(FP8X4), rhs_scale=x2_s[:], start=True, stop=False,
            )
        logarithm(0)
        sums(1)
        quantise_z(0)
        second_product(0)
        logarithm(1)
        quantise_z(1)
        second_product(1)

        top = [sb(f"top{t}", [P, 1], F32) for t in range(PACK)]
        shift = [sb(f"shift{t}", [P, 1], F32) for t in range(PACK)]
        for t in range(PACK):
            nc.vector.tensor_scalar(out=h[t][:, :S], in0=h_ps[t][:], scalar1=1.0, scalar2=None, op0=ALU.mult, op1=ALU.max, accum_out=top[t][:])
            nc.vector.tensor_scalar(out=shift[t][:], in0=top[t][:], scalar1=minus_tau[:, t : t + 1], scalar2=None, op0=ALU.mult)

        larger = [sb(f"larger{t}", [P, S], F32) for t in range(PACK)]
        for t in range(PACK):
            ea = sb(f"ea{t}", [P, S], F32)
            nc.scalar.activation(ea[:], h[t][:].indirect(n2_sb[:]), ACT.Exp, bias=shift[t][:], scale=tau_sb[:, t : t + 1])
            nc.vector.scalar_tensor_tensor(larger[t][:], ea[:], 2.0, h[t][:, :S], ALU.mult, ALU.max)
        other = sb(f"top{PACK - 1}", [P, 2, PACK, HALF], F32)
        codes = sb("codes", [P, S], U32)
        code_scales = sb("code_scales", [P, S], U8)
        out_rows = out_0.rearrange("(p t) j -> p t j", t=PACK)
        out_words = out_1[0].rearrange("p n t -> p (n t)").bitcast(I32)
        for half in range(2):
            js = slice(half * HALF, (half + 1) * HALF)
            ls = slice(half * HALF // 16, (half + 1) * HALF // 16)
            result = sb(f"result{half}", [P, PACK, HALF], F32)
            for t in range(PACK):
                nc.scalar.activation(other[:, half, t, :], h[t][:].indirect(n3_sb[:, ls]), ACT.Copy)
                nc.vector.scalar_tensor_tensor(result[:, t, :], other[:, half, t, :], -0.5, larger[t][:, js], ALU.mult, ALU.add)
            nc.sync.dma_start(out=out_rows[:, :, js], in_=result[:])
            rounded = sb(f"rounded{half}", [P, HALF, PACK], BF16)
            nc.vector.tensor_copy(out=rounded[:], in_=result[:].rearrange("p t j -> p j t"))
            nc.vector.quantize_mx(out=codes[:, js].bitcast(FP8X4), scales=code_scales[:, js], in_=rounded[:].rearrange("p j t -> p (j t)"))
            nc.sync.dma_start(out=out_words[:, js], in_=codes[:, js].bitcast(I32))
        for quad in range(4):
            queue = nc.scalar if quad < 2 else nc.sync
            queue.dma_start(
                out=out_2[0, 4 * quad : 4 * quad + 4, :].bitcast(I32), in_=code_scales[32 * quad : 32 * quad + 4, :].bitcast(I32)
            )
